import numpy as np
import ml_dtypes


def mxq(x, axis, fmt="e4m3"):
    dtype, down = {"e4m3": (ml_dtypes.float8_e4m3fn, 7), "e5m2": (ml_dtypes.float8_e5m2, 14)}[fmt]
    v = np.moveaxis(np.asarray(x, np.float32).astype(ml_dtypes.bfloat16).astype(np.float64), axis, -1)
    blocks = v.reshape(v.shape[:-1] + (-1, 32))
    amax = np.abs(blocks).max(-1, keepdims=True)
    byte = np.maximum(np.where(amax > 0, np.frexp(amax)[1] - 1 + 127, 0) - down, 1)
    scale = np.exp2(byte - 127.0)
    codes = (blocks / scale).astype(np.float32).astype(dtype).astype(np.float64)
    return np.moveaxis((codes * scale).reshape(v.shape), -1, axis)


WIDE = False


def mx_kscale(k):
    if not WIDE:
        return np.ones(k)
    levels = np.array([10, -10, 5, -5, 0])
    if k % 512:
        return np.exp2(np.random.permutation(np.resize(levels, k // 32))).repeat(32)
    a = np.empty((k // 512, 16))
    for p in range(k // 512):
        a[p, :8] = np.random.permutation(np.resize(levels, 8))
        for g in range(8):
            far = levels[np.abs(levels - a[p, g]) >= 10]
            a[p, g + 8] = far[np.random.randint(len(far))]
    return np.exp2(a.ravel()).repeat(32)


def f64(x):
    return np.asarray(x).astype(np.float64)


def striped(idx):
    return np.tile(idx.reshape(-1, 16).T, (8, 1)).astype(np.uint16)


def unstriped(offs):
    return offs[:16].T.reshape(-1).astype(np.int64)


def pack_weight(w):
    k, n = w.shape
    w = f64(np.asarray(w, np.float32).astype(ml_dtypes.bfloat16)).reshape(k // 32, 32, n)
    amax = np.abs(w).max(1)
    byte = np.clip(np.where(amax > 0, np.frexp(amax)[1] - 1 + 127 - 7, 1), 1, 254)
    scaled = (w * np.exp2(127.0 - byte)[:, None, :]).reshape(k, n).astype(np.float32)
    words = np.ascontiguousarray(scaled.reshape(k // 512, 128, 4, n).transpose(0, 1, 3, 2)).astype(ml_dtypes.float8_e4m3fn).view(np.uint8)
    return words, np.ascontiguousarray(byte.astype(np.uint8).reshape(k // 512, 16, n))


def unpack_weight(words, scales):
    g, p, n, _ = words.shape
    vals = np.ascontiguousarray(words).view(ml_dtypes.float8_e4m3fn).astype(np.float64) * np.repeat(np.exp2(scales.astype(np.float64) - 127.0), 8, axis=1)[..., None]
    return vals.transpose(0, 1, 3, 2).reshape(g * 512, n)


K, T, S, N, V = 512, 2048, 512, 128, 256
P = 2 ** 7


def setup_inputs():
    n = np.random.standard_normal
    s = mx_kscale(K)[:, None]
    packed_xT = pack_weight(n((K, T)) * s)
    return {
        "x_words": packed_xT[0],
        "x_scales": packed_xT[1],
        "w1": (n((K, N)) / np.sqrt(K) / s).astype(np.float32),
        "hist": (1.5 * n((N, V))).astype(np.float32),
        "alpha": (np.tile(np.random.uniform(0.1, 0.5, V), (P, 1))).astype(np.float32),
        "offs": striped(np.random.permutation(T)[:S]),
        "pos1": striped(np.random.permutation(S)[:V]),
        "pos2": striped(np.random.permutation(S)[:V]),
        "pos3": striped(np.random.permutation(S)[:V]),
        "cen": striped(np.random.permutation(S)[:V]),
    }


def reference(x_words, x_scales, w1, hist, alpha, offs, pos1, pos2, pos3, cen):
    xq = unpack_weight(x_words, x_scales)[:, unstriped(offs)]
    y = mxq(f64(w1), 0, "e4m3").T @ xq
    g0 = y[:, unstriped(pos1)]
    g1 = y[:, unstriped(pos2)]
    g2 = y[:, unstriped(pos3)]
    mu = (g0 + g1 + g2) / 3
    sd = np.sqrt(((g0 - mu) ** 2 + (g1 - mu) ** 2 + (g2 - mu) ** 2) / 3 + 0.01)
    cl = np.maximum(np.minimum(f64(hist), mu + sd), mu - sd)
    return cl + f64(alpha)[:1] * (y[:, unstriped(cen)] - cl)

@@ -1,0 +1,142 @@
+import math
+from contextlib import ExitStack
+
+import concourse.mybir as mybir
+
+K, T, S, N, V = 512, 2048, 512, 128, 256
+P = 128
+PACK = 4
+FLOPS = 2 * K * N * S
+
+F32 = mybir.dt.float32
+BF16 = mybir.dt.bfloat16
+I32 = mybir.dt.int32
+U32 = mybir.dt.uint32
+U16 = mybir.dt.uint16
+U8 = mybir.dt.uint8
+FP8X4 = mybir.dt.float8_e4m3fn_x4
+ALU = mybir.AluOpType
+ACT = mybir.ActivationFunctionType
+
+
+def tile_picked_ytaa_mix_p_kernel(
+    tc, x_words, x_scales, w1, hist, alpha, offs, pos1, pos2, pos3, cen, out
+):
+    nc = tc.nc
+    with ExitStack() as ctx:
+        keep = ctx.enter_context(tc.tile_pool(name="keep", bufs=1))
+        psum = ctx.enter_context(tc.psum_pool(name="psum", bufs=1))
+
+        scale_table = keep.tile([P, T], U8, name="scale_table", align_bytes=64)
+        nc.vector.memset(scale_table[:].bitcast(I32), 0)
+        warm = keep.tile([P, 8], F32, name="warm")
+        nc.vector.memset(warm[:], 1.0)
+
+        offs_sb = keep.tile([P, S // 16], U16, name="offs_sb")
+        nc.sync.dma_start(offs_sb[:], offs)
+        w_raw = keep.tile([P, PACK, N], F32, name="w_raw")
+        nc.sync.dma_start(w_raw[:], w1.rearrange("(p j) n -> p j n", j=PACK))
+        for q in range(4):
+            nc.scalar.dma_start(
+                scale_table[32 * q : 32 * q + 4, :].bitcast(I32),
+                x_scales[0, 4 * q : 4 * q + 4, :].bitcast(I32),
+            )
+        word_table = keep.tile([P, T], I32, name="word_table", align_bytes=64)
+        nc.sync.dma_start(word_table[:], x_words[0].rearrange("p c r -> p (c r)").bitcast(I32))
+
+        lists = {}
+        for name, src in (("pos2", pos2), ("pos3", pos3), ("pos1", pos1), ("cen", cen)):
+            lists[name] = keep.tile([P, V // 16], U16, name=name + "_sb")
+            nc.sync.dma_start(lists[name][:], src)
+        hist_sb = keep.tile([P, V], F32, name="hist_sb")
+        nc.sync.dma_start(hist_sb[:], hist)
+        alpha_sb = keep.tile([P, V], F32, name="alpha_sb")
+        nc.sync.dma_start(alpha_sb[:], alpha)
+
+        warm_out = keep.tile([P, 8], F32, name="warm_out")
+        nc.scalar.activation(warm_out[:], warm[:], ACT.Sqrt)
+
+        w_grouped = keep.tile([P, N, PACK], BF16, name="w_grouped", align_bytes=64)
+        nc.scalar.copy(w_grouped[:], w_raw[:].rearrange("p j n -> p n j"))
+
+        picked_scales = keep.tile([P, S], U8, name="picked_scales", align_bytes=64)
+        nc.vector.tensor_copy(picked_scales[:], scale_table[:].indirect(offs_sb[:]))
+
+        w_codes = keep.tile([P, N], U32, name="w_codes", align_bytes=64)
+        w_scales = keep.tile([P, N], U8, name="w_scales", align_bytes=64)
+        nc.vector.quantize_mx(
+            out=w_codes[:].bitcast(FP8X4),
+            scales=w_scales[:],
+            in_=w_grouped[:].rearrange("p n j -> p (n j)"),
+        )
+
+        y = keep.tile([P, S], F32, name="y")
+        H = S // 2
+        picked = []
+        for h in range(2):
+            t = keep.tile([P, H], U32, name="picked_words%d" % h, align_bytes=64)
+            nc.vector.tensor_copy(
+                t[:], word_table[:].bitcast(U32).indirect(offs_sb[:, h * 16 : (h + 1) * 16])
+            )
+            picked.append(t)
+        for h, c0, width, eng in ((0, 0, 256, "s"), (1, 0, 128, "v"), (1, 128, 128, "s")):
+            acc = psum.tile([P, width], F32, name="acc%d_%d" % (h, c0))
+            col = h * H + c0
+            nc.tensor.matmul_mx(
+                out=acc[:],
+                lhsT=w_codes[:].bitcast(FP8X4),
+                lhsT_scale=w_scales[:],
+                rhs=picked[h][:, c0 : c0 + width].bitcast(FP8X4),
+                rhs_scale=picked_scales[:, col : col + width],
+                start=True,
+                stop=True,
+            )
+            if eng == "s":
+                nc.scalar.copy(y[:, col : col + width], acc[:])
+            else:
+                nc.vector.tensor_copy(y[:, col : col + width], acc[:])
+
+        keep_share = keep.tile([P, V], F32, name="keep_share")
+        nc.scalar.activation(keep_share[:], alpha_sb[:], ACT.Copy, bias=1.0, scale=-1.0)
+
+        W = V // 2
+        names = ("b", "t", "m", "u", "ayc", "t2", "u2", "var", "sd", "mu", "d", "x1", "x2", "cl", "kc", "res")
+        tl = [{n: keep.tile([P, W], F32, name="%s%d" % (n, h)) for n in names} for h in range(2)]
+
+        def gathered(name, h):
+            return y[:].indirect(lists[name][:, h * 8 : (h + 1) * 8])
+
+        def cols(tile, h):
+            return tile[:, h * W : (h + 1) * W]
+
+        vec = nc.vector
+        for h in range(2):
+            vec.tensor_copy(tl[h]["b"][:], gathered("pos2", h))
+        for h in range(2):
+            vec.tensor_tensor(tl[h]["t"][:], gathered("pos3", h), tl[h]["b"][:], ALU.subtract)
+            nc.scalar.activation(tl[h]["t2"][:], tl[h]["t"][:], ACT.Square, scale=math.sqrt(1.0 / 6.0))
+        for h in range(2):
+            vec.scalar_tensor_tensor(tl[h]["m"][:], tl[h]["t"][:], 0.5, tl[h]["b"][:], ALU.mult, ALU.add)
+        for h in range(2):
+            vec.tensor_tensor(tl[h]["u"][:], gathered("pos1", h), tl[h]["m"][:], ALU.subtract)
+            nc.scalar.activation(tl[h]["u2"][:], tl[h]["u"][:], ACT.Square, scale=math.sqrt(2.0 / 9.0))
+        for h in range(2):
+            vec.scalar_tensor_tensor(tl[h]["mu"][:], tl[h]["u"][:], 1.0 / 3.0, tl[h]["m"][:], ALU.mult, ALU.add)
+        for h in range(2):
+            vec.scalar_tensor_tensor(tl[h]["var"][:], tl[h]["t2"][:], 0.01, tl[h]["u2"][:], ALU.add, ALU.add)
+            nc.scalar.activation(tl[h]["sd"][:], tl[h]["var"][:], ACT.Sqrt)
+        for h in range(2):
+            vec.tensor_tensor(tl[h]["d"][:], cols(hist_sb, h), tl[h]["mu"][:], ALU.subtract)
+        for h in range(2):
+            vec.tensor_tensor(tl[h]["ayc"][:], gathered("cen", h), cols(alpha_sb, h), ALU.mult)
+        for h in range(2):
+            vec.tensor_tensor(tl[h]["x1"][:], tl[h]["d"][:], tl[h]["sd"][:], ALU.min)
+        for h in range(2):
+            vec.scalar_tensor_tensor(tl[h]["x2"][:], tl[h]["sd"][:], -1.0, tl[h]["x1"][:], ALU.mult, ALU.max)
+        for h in range(2):
+            vec.tensor_tensor(tl[h]["cl"][:], tl[h]["x2"][:], tl[h]["mu"][:], ALU.add)
+        for h in range(2):
+            vec.tensor_tensor(tl[h]["kc"][:], tl[h]["cl"][:], cols(keep_share, h), ALU.mult)
+        for h in range(2):
+            vec.tensor_tensor(tl[h]["res"][:], tl[h]["kc"][:], tl[h]["ayc"][:], ALU.add)
+            nc.sync.dma_start(out[:, h * W : (h + 1) * W], tl[h]["res"][:])

@@ -37,7 +37,7 @@ def tile_picked_ytaa_mix_p_kernel(
         w_raw = keep.tile([P, PACK, N], F32, name="w_raw")
         nc.sync.dma_start(w_raw[:], w1.rearrange("(p j) n -> p j n", j=PACK))
         for q in range(4):
-            nc.scalar.dma_start(
+            (nc.sync if q < 2 else nc.scalar).dma_start(
                 scale_table[32 * q : 32 * q + 4, :].bitcast(I32),
                 x_scales[0, 4 * q : 4 * q + 4, :].bitcast(I32),
             )
@@ -57,7 +57,7 @@ def tile_picked_ytaa_mix_p_kernel(
         nc.scalar.activation(warm_out[:], warm[:], ACT.Sqrt)
 
         w_grouped = keep.tile([P, N, PACK], BF16, name="w_grouped", align_bytes=64)
-        nc.scalar.copy(w_grouped[:], w_raw[:].rearrange("p j n -> p n j"))
+        nc.vector.tensor_copy(w_grouped[:], w_raw[:].rearrange("p j n -> p n j"))
 
         picked_scales = keep.tile([P, S], U8, name="picked_scales", align_bytes=64)
         nc.vector.tensor_copy(picked_scales[:], scale_table[:].indirect(offs_sb[:]))
@@ -100,7 +100,7 @@ def tile_picked_ytaa_mix_p_kernel(
         nc.scalar.activation(keep_share[:], alpha_sb[:], ACT.Copy, bias=1.0, scale=-1.0)
 
         W = V // 2
-        names = ("b", "t", "m", "u", "ayc", "t2", "u2", "var", "sd", "mu", "d", "x1", "x2", "cl", "kc", "res")
+        names = ("b", "t", "m", "u", "t2", "u2", "var", "sd", "mu", "d", "x1", "x2", "cl", "kc", "res")
         tl = [{n: keep.tile([P, W], F32, name="%s%d" % (n, h)) for n in names} for h in range(2)]
 
         def gathered(name, h):
@@ -128,6 +128,7 @@ def tile_picked_ytaa_mix_p_kernel(
         for h in range(2):
             vec.tensor_tensor(tl[h]["d"][:], cols(hist_sb, h), tl[h]["mu"][:], ALU.subtract)
         for h in range(2):
+            tl[h]["ayc"] = keep.tile([P, W], F32, name="t2%d" % h)
             vec.tensor_tensor(tl[h]["ayc"][:], gathered("cen", h), cols(alpha_sb, h), ALU.mult)
         for h in range(2):
             vec.tensor_tensor(tl[h]["x1"][:], tl[h]["d"][:], tl[h]["sd"][:], ALU.min)

@@ -37,21 +37,21 @@ def tile_picked_ytaa_mix_p_kernel(
         w_raw = keep.tile([P, PACK, N], F32, name="w_raw")
         nc.sync.dma_start(w_raw[:], w1.rearrange("(p j) n -> p j n", j=PACK))
         for q in range(4):
-            (nc.sync if q < 2 else nc.scalar).dma_start(
+            nc.sync.dma_start(
                 scale_table[32 * q : 32 * q + 4, :].bitcast(I32),
                 x_scales[0, 4 * q : 4 * q + 4, :].bitcast(I32),
             )
         word_table = keep.tile([P, T], I32, name="word_table", align_bytes=64)
         nc.sync.dma_start(word_table[:], x_words[0].rearrange("p c r -> p (c r)").bitcast(I32))
 
+        alpha_sb = keep.tile([P, V], F32, name="alpha_sb")
+        nc.sync.dma_start(alpha_sb[:], alpha)
+        hist_sb = keep.tile([P, V], F32, name="hist_sb")
+        nc.sync.dma_start(hist_sb[:], hist)
         lists = {}
         for name, src in (("pos2", pos2), ("pos3", pos3), ("pos1", pos1), ("cen", cen)):
             lists[name] = keep.tile([P, V // 16], U16, name=name + "_sb")
             nc.sync.dma_start(lists[name][:], src)
-        hist_sb = keep.tile([P, V], F32, name="hist_sb")
-        nc.sync.dma_start(hist_sb[:], hist)
-        alpha_sb = keep.tile([P, V], F32, name="alpha_sb")
-        nc.sync.dma_start(alpha_sb[:], alpha)
 
         warm_out = keep.tile([P, 8], F32, name="warm_out")
         nc.scalar.activation(warm_out[:], warm[:], ACT.Sqrt)

@@ -1,12 +1,24 @@
-import math
 from contextlib import ExitStack
 
 import concourse.mybir as mybir
 
 K, T, S, N, V = 512, 2048, 512, 128, 256
+FLOPS = 2 * K * N * S
+
 P = 128
 PACK = 4
-FLOPS = 2 * K * N * S
+QUADRANT = 32
+SCALE_ROWS = 4
+PER_COLUMN = 16
+EPS = 0.01
+VARIANCE_FACTOR = 2.0 / 9.0
+SPREAD_FACTOR = 3.0 / 4.0
+
+WORD_HALF = S // 2
+PRODUCTS = ((0, 0, WORD_HALF), (1, 0, WORD_HALF // 2), (1, WORD_HALF // 2, WORD_HALF // 2))
+PRODUCT_ON_VECTOR = 1
+HALVES = ((0, 128), (128, 256))
+THIRDS = ((0, 96), (96, 176), (176, 256))
 
 F32 = mybir.dt.float32
 BF16 = mybir.dt.bfloat16
@@ -29,32 +41,31 @@ def tile_picked_ytaa_mix_p_kernel(
 
         scale_table = keep.tile([P, T], U8, name="scale_table", align_bytes=64)
         nc.vector.memset(scale_table[:].bitcast(I32), 0)
-        warm = keep.tile([P, 8], F32, name="warm")
-        nc.vector.memset(warm[:], 1.0)
+        one = keep.tile([P, 1], F32, name="one")
+        nc.vector.memset(one[:], 1.0)
 
-        offs_sb = keep.tile([P, S // 16], U16, name="offs_sb")
-        nc.sync.dma_start(offs_sb[:], offs)
         w_raw = keep.tile([P, PACK, N], F32, name="w_raw")
         nc.sync.dma_start(w_raw[:], w1.rearrange("(p j) n -> p j n", j=PACK))
-        for q in range(4):
+        offs_sb = keep.tile([P, S // PER_COLUMN], U16, name="offs_sb")
+        nc.sync.dma_start(offs_sb[:], offs)
+        for q in range(P // QUADRANT):
             nc.sync.dma_start(
-                scale_table[32 * q : 32 * q + 4, :].bitcast(I32),
-                x_scales[0, 4 * q : 4 * q + 4, :].bitcast(I32),
+                scale_table[QUADRANT * q : QUADRANT * q + SCALE_ROWS, :].bitcast(I32),
+                x_scales[0, SCALE_ROWS * q : SCALE_ROWS * (q + 1), :].bitcast(I32),
             )
         word_table = keep.tile([P, T], I32, name="word_table", align_bytes=64)
         nc.sync.dma_start(word_table[:], x_words[0].rearrange("p c r -> p (c r)").bitcast(I32))
-
         alpha_sb = keep.tile([P, V], F32, name="alpha_sb")
         nc.sync.dma_start(alpha_sb[:], alpha)
         hist_sb = keep.tile([P, V], F32, name="hist_sb")
         nc.sync.dma_start(hist_sb[:], hist)
         lists = {}
         for name, src in (("pos2", pos2), ("pos3", pos3), ("pos1", pos1), ("cen", cen)):
-            lists[name] = keep.tile([P, V // 16], U16, name=name + "_sb")
+            lists[name] = keep.tile([P, V // PER_COLUMN], U16, name=name + "_sb")
             nc.sync.dma_start(lists[name][:], src)
 
-        warm_out = keep.tile([P, 8], F32, name="warm_out")
-        nc.scalar.activation(warm_out[:], warm[:], ACT.Sqrt)
+        root_spread = keep.tile([P, 1], F32, name="root_spread")
+        nc.scalar.activation(root_spread[:], one[:], ACT.Sqrt, scale=SPREAD_FACTOR)
 
         w_grouped = keep.tile([P, N, PACK], BF16, name="w_grouped", align_bytes=64)
         nc.vector.tensor_copy(w_grouped[:], w_raw[:].rearrange("p j n -> p n j"))
@@ -70,74 +81,81 @@ def tile_picked_ytaa_mix_p_kernel(
             in_=w_grouped[:].rearrange("p n j -> p (n j)"),
         )
 
+        picked_words = []
+        half_columns = WORD_HALF // PER_COLUMN
+        for half in range(S // WORD_HALF):
+            words = keep.tile([P, WORD_HALF], U32, name="picked_words%d" % half, align_bytes=64)
+            offsets = offs_sb[:, half * half_columns : (half + 1) * half_columns]
+            nc.vector.tensor_copy(words[:], word_table[:].bitcast(U32).indirect(offsets))
+            picked_words.append(words)
+
         y = keep.tile([P, S], F32, name="y")
-        H = S // 2
-        picked = []
-        for h in range(2):
-            t = keep.tile([P, H], U32, name="picked_words%d" % h, align_bytes=64)
-            nc.vector.tensor_copy(
-                t[:], word_table[:].bitcast(U32).indirect(offs_sb[:, h * 16 : (h + 1) * 16])
-            )
-            picked.append(t)
-        for h, c0, width, eng in ((0, 0, 256, "s"), (1, 0, 128, "v"), (1, 128, 128, "s")):
-            acc = psum.tile([P, width], F32, name="acc%d_%d" % (h, c0))
-            col = h * H + c0
+        for index, (half, first, width) in enumerate(PRODUCTS):
+            acc = psum.tile([P, width], F32, name="acc%d" % index)
+            cols = slice(half * WORD_HALF + first, half * WORD_HALF + first + width)
             nc.tensor.matmul_mx(
                 out=acc[:],
                 lhsT=w_codes[:].bitcast(FP8X4),
                 lhsT_scale=w_scales[:],
-                rhs=picked[h][:, c0 : c0 + width].bitcast(FP8X4),
-                rhs_scale=picked_scales[:, col : col + width],
+                rhs=picked_words[half][:, first : first + width].bitcast(FP8X4),
+                rhs_scale=picked_scales[:, cols],
                 start=True,
                 stop=True,
             )
-            if eng == "s":
-                nc.scalar.copy(y[:, col : col + width], acc[:])
+            if index == PRODUCT_ON_VECTOR:
+                nc.vector.tensor_copy(y[:, cols], acc[:])
             else:
-                nc.vector.tensor_copy(y[:, col : col + width], acc[:])
+                nc.scalar.copy(y[:, cols], acc[:])
 
-        keep_share = keep.tile([P, V], F32, name="keep_share")
-        nc.scalar.activation(keep_share[:], alpha_sb[:], ACT.Copy, bias=1.0, scale=-1.0)
+        old_share = keep.tile([P, V], F32, name="old_share")
+        nc.scalar.activation(old_share[:], alpha_sb[:], ACT.Copy, bias=1.0, scale=-1.0)
 
-        W = V // 2
-        names = ("b", "t", "m", "u", "t2", "u2", "var", "sd", "mu", "d", "x1", "x2", "cl", "kc", "res")
-        tl = [{n: keep.tile([P, W], F32, name="%s%d" % (n, h)) for n in names} for h in range(2)]
+        def pixels(name):
+            return keep.tile([P, V], F32, name=name)
 
-        def gathered(name, h):
-            return y[:].indirect(lists[name][:, h * 8 : (h + 1) * 8])
+        def looked_up(name, lo, hi):
+            return y[:].indirect(lists[name][:, lo // PER_COLUMN : hi // PER_COLUMN])
 
-        def cols(tile, h):
-            return tile[:, h * W : (h + 1) * W]
+        second, spread, mid, off = pixels("second"), pixels("spread"), pixels("mid"), pixels("off")
+        spread_sq, off_sq = pixels("spread_sq"), pixels("off_sq")
+        squares, sd, mean, gap = pixels("squares"), pixels("sd"), pixels("mean"), pixels("gap")
+        capped, clamped = pixels("capped"), pixels("clamped")
+        clipped, old_part, result = pixels("clipped"), pixels("old_part"), pixels("result")
 
         vec = nc.vector
-        for h in range(2):
-            vec.tensor_copy(tl[h]["b"][:], gathered("pos2", h))
-        for h in range(2):
-            vec.tensor_tensor(tl[h]["t"][:], gathered("pos3", h), tl[h]["b"][:], ALU.subtract)
-            nc.scalar.activation(tl[h]["t2"][:], tl[h]["t"][:], ACT.Square, scale=math.sqrt(1.0 / 6.0))
-        for h in range(2):
-            vec.scalar_tensor_tensor(tl[h]["m"][:], tl[h]["t"][:], 0.5, tl[h]["b"][:], ALU.mult, ALU.add)
-        for h in range(2):
-            vec.tensor_tensor(tl[h]["u"][:], gathered("pos1", h), tl[h]["m"][:], ALU.subtract)
-            nc.scalar.activation(tl[h]["u2"][:], tl[h]["u"][:], ACT.Square, scale=math.sqrt(2.0 / 9.0))
-        for h in range(2):
-            vec.scalar_tensor_tensor(tl[h]["mu"][:], tl[h]["u"][:], 1.0 / 3.0, tl[h]["m"][:], ALU.mult, ALU.add)
-        for h in range(2):
-            vec.scalar_tensor_tensor(tl[h]["var"][:], tl[h]["t2"][:], 0.01, tl[h]["u2"][:], ALU.add, ALU.add)
-            nc.scalar.activation(tl[h]["sd"][:], tl[h]["var"][:], ACT.Sqrt)
-        for h in range(2):
-            vec.tensor_tensor(tl[h]["d"][:], cols(hist_sb, h), tl[h]["mu"][:], ALU.subtract)
-        for h in range(2):
-            tl[h]["ayc"] = keep.tile([P, W], F32, name="t2%d" % h)
-            vec.tensor_tensor(tl[h]["ayc"][:], gathered("cen", h), cols(alpha_sb, h), ALU.mult)
-        for h in range(2):
-            vec.tensor_tensor(tl[h]["x1"][:], tl[h]["d"][:], tl[h]["sd"][:], ALU.min)
-        for h in range(2):
-            vec.scalar_tensor_tensor(tl[h]["x2"][:], tl[h]["sd"][:], -1.0, tl[h]["x1"][:], ALU.mult, ALU.max)
-        for h in range(2):
-            vec.tensor_tensor(tl[h]["cl"][:], tl[h]["x2"][:], tl[h]["mu"][:], ALU.add)
-        for h in range(2):
-            vec.tensor_tensor(tl[h]["kc"][:], tl[h]["cl"][:], cols(keep_share, h), ALU.mult)
-        for h in range(2):
-            vec.tensor_tensor(tl[h]["res"][:], tl[h]["kc"][:], tl[h]["ayc"][:], ALU.add)
-            nc.sync.dma_start(out[:, h * W : (h + 1) * W], tl[h]["res"][:])
+        for lo, hi in HALVES:
+            vec.tensor_copy(second[:, lo:hi], looked_up("pos2", lo, hi))
+        for lo, hi in HALVES:
+            vec.tensor_tensor(spread[:, lo:hi], looked_up("pos3", lo, hi), second[:, lo:hi], ALU.subtract)
+            nc.scalar.activation(spread_sq[:, lo:hi], spread[:, lo:hi], ACT.Square, scale=root_spread[:])
+        for lo, hi in HALVES:
+            vec.scalar_tensor_tensor(mid[:, lo:hi], spread[:, lo:hi], 0.5, second[:, lo:hi], ALU.mult, ALU.add)
+        for lo, hi in HALVES:
+            vec.tensor_tensor(off[:, lo:hi], looked_up("pos1", lo, hi), mid[:, lo:hi], ALU.subtract)
+            nc.scalar.activation(off_sq[:, lo:hi], off[:, lo:hi], ACT.Square)
+        for lo, hi in HALVES:
+            vec.scalar_tensor_tensor(mean[:, lo:hi], off[:, lo:hi], 1.0 / 3.0, mid[:, lo:hi], ALU.mult, ALU.add)
+        for lo, hi in THIRDS:
+            vec.scalar_tensor_tensor(
+                squares[:, lo:hi], spread_sq[:, lo:hi], EPS / VARIANCE_FACTOR, off_sq[:, lo:hi], ALU.add, ALU.add
+            )
+            nc.scalar.activation(sd[:, lo:hi], squares[:, lo:hi], ACT.Sqrt, scale=VARIANCE_FACTOR)
+        for lo, hi in HALVES:
+            vec.tensor_tensor(gap[:, lo:hi], hist_sb[:, lo:hi], mean[:, lo:hi], ALU.subtract)
+
+        new_part = mid
+        vec.tensor_tensor(new_part[:], looked_up("cen", 0, V), alpha_sb[:], ALU.mult)
+
+        for lo, hi in THIRDS:
+            vec.tensor_tensor(capped[:, lo:hi], gap[:, lo:hi], sd[:, lo:hi], ALU.min)
+        for lo, hi in THIRDS:
+            vec.scalar_tensor_tensor(clamped[:, lo:hi], sd[:, lo:hi], -1.0, capped[:, lo:hi], ALU.mult, ALU.max)
+        for lo, hi in THIRDS:
+            vec.tensor_tensor(clipped[:, lo:hi], clamped[:, lo:hi], mean[:, lo:hi], ALU.add)
+        for lo, hi in THIRDS:
+            vec.tensor_tensor(old_part[:, lo:hi], clipped[:, lo:hi], old_share[:, lo:hi], ALU.mult)
+        for lo, hi in THIRDS:
+            vec.tensor_tensor(result[:, lo:hi], old_part[:, lo:hi], new_part[:, lo:hi], ALU.add)
+
+        for lo, hi in HALVES:
+            nc.sync.dma_start(out[:, lo:hi], result[:, lo:hi])

from contextlib import ExitStack

import concourse.mybir as mybir

K, T, S, N, V = 512, 2048, 512, 128, 256
FLOPS = 2 * K * N * S

P = 128
PACK = 4
QUADRANT = 32
SCALE_ROWS = 4
PER_COLUMN = 16
EPS = 0.01
VARIANCE_FACTOR = 2.0 / 9.0
SPREAD_FACTOR = 3.0 / 4.0

WORD_HALF = S // 2
PRODUCTS = ((0, 0, WORD_HALF), (1, 0, WORD_HALF // 2), (1, WORD_HALF // 2, WORD_HALF // 2))
PRODUCT_ON_VECTOR = 1
HALVES = ((0, 128), (128, 256))
THIRDS = ((0, 96), (96, 176), (176, 256))

F32 = mybir.dt.float32
BF16 = mybir.dt.bfloat16
I32 = mybir.dt.int32
U32 = mybir.dt.uint32
U16 = mybir.dt.uint16
U8 = mybir.dt.uint8
FP8X4 = mybir.dt.float8_e4m3fn_x4
ALU = mybir.AluOpType
ACT = mybir.ActivationFunctionType


def tile_picked_ytaa_mix_p_kernel(
    tc, x_words, x_scales, w1, hist, alpha, offs, pos1, pos2, pos3, cen, out
):
    nc = tc.nc
    with ExitStack() as ctx:
        keep = ctx.enter_context(tc.tile_pool(name="keep", bufs=1))
        psum = ctx.enter_context(tc.psum_pool(name="psum", bufs=1))

        scale_table = keep.tile([P, T], U8, name="scale_table", align_bytes=64)
        nc.vector.memset(scale_table[:].bitcast(I32), 0)
        one = keep.tile([P, 1], F32, name="one")
        nc.vector.memset(one[:], 1.0)

        w_raw = keep.tile([P, PACK, N], F32, name="w_raw")
        nc.sync.dma_start(w_raw[:], w1.rearrange("(p j) n -> p j n", j=PACK))
        offs_sb = keep.tile([P, S // PER_COLUMN], U16, name="offs_sb")
        nc.sync.dma_start(offs_sb[:], offs)
        for q in range(P // QUADRANT):
            nc.sync.dma_start(
                scale_table[QUADRANT * q : QUADRANT * q + SCALE_ROWS, :].bitcast(I32),
                x_scales[0, SCALE_ROWS * q : SCALE_ROWS * (q + 1), :].bitcast(I32),
            )
        word_table = keep.tile([P, T], I32, name="word_table", align_bytes=64)
        nc.sync.dma_start(word_table[:], x_words[0].rearrange("p c r -> p (c r)").bitcast(I32))
        alpha_sb = keep.tile([P, V], F32, name="alpha_sb")
        nc.sync.dma_start(alpha_sb[:], alpha)
        hist_sb = keep.tile([P, V], F32, name="hist_sb")
        nc.sync.dma_start(hist_sb[:], hist)
        lists = {}
        for name, src in (("pos2", pos2), ("pos3", pos3), ("pos1", pos1), ("cen", cen)):
            lists[name] = keep.tile([P, V // PER_COLUMN], U16, name=name + "_sb")
            nc.sync.dma_start(lists[name][:], src)

        root_spread = keep.tile([P, 1], F32, name="root_spread")
        nc.scalar.activation(root_spread[:], one[:], ACT.Sqrt, scale=SPREAD_FACTOR)

        w_grouped = keep.tile([P, N, PACK], BF16, name="w_grouped", align_bytes=64)
        nc.vector.tensor_copy(w_grouped[:], w_raw[:].rearrange("p j n -> p n j"))

        picked_scales = keep.tile([P, S], U8, name="picked_scales", align_bytes=64)
        nc.vector.tensor_copy(picked_scales[:], scale_table[:].indirect(offs_sb[:]))

        w_codes = keep.tile([P, N], U32, name="w_codes", align_bytes=64)
        w_scales = keep.tile([P, N], U8, name="w_scales", align_bytes=64)
        nc.vector.quantize_mx(
            out=w_codes[:].bitcast(FP8X4),
            scales=w_scales[:],
            in_=w_grouped[:].rearrange("p n j -> p (n j)"),
        )

        picked_words = []
        half_columns = WORD_HALF // PER_COLUMN
        for half in range(S // WORD_HALF):
            words = keep.tile([P, WORD_HALF], U32, name="picked_words%d" % half, align_bytes=64)
            offsets = offs_sb[:, half * half_columns : (half + 1) * half_columns]
            nc.vector.tensor_copy(words[:], word_table[:].bitcast(U32).indirect(offsets))
            picked_words.append(words)

        y = keep.tile([P, S], F32, name="y")
        for index, (half, first, width) in enumerate(PRODUCTS):
            acc = psum.tile([P, width], F32, name="acc%d" % index)
            cols = slice(half * WORD_HALF + first, half * WORD_HALF + first + width)
            nc.tensor.matmul_mx(
                out=acc[:],
                lhsT=w_codes[:].bitcast(FP8X4),
                lhsT_scale=w_scales[:],
                rhs=picked_words[half][:, first : first + width].bitcast(FP8X4),
                rhs_scale=picked_scales[:, cols],
                start=True,
                stop=True,
            )
            if index == PRODUCT_ON_VECTOR:
                nc.vector.tensor_copy(y[:, cols], acc[:])
            else:
                nc.scalar.copy(y[:, cols], acc[:])

        old_share = keep.tile([P, V], F32, name="old_share")
        nc.scalar.activation(old_share[:], alpha_sb[:], ACT.Copy, bias=1.0, scale=-1.0)

        def pixels(name):
            return keep.tile([P, V], F32, name=name)

        def looked_up(name, lo, hi):
            return y[:].indirect(lists[name][:, lo // PER_COLUMN : hi // PER_COLUMN])

        second, spread, mid, off = pixels("second"), pixels("spread"), pixels("mid"), pixels("off")
        spread_sq, off_sq = pixels("spread_sq"), pixels("off_sq")
        squares, sd, mean, gap = pixels("squares"), pixels("sd"), pixels("mean"), pixels("gap")
        capped, clamped = pixels("capped"), pixels("clamped")
        clipped, old_part, result = pixels("clipped"), pixels("old_part"), pixels("result")

        vec = nc.vector
        for lo, hi in HALVES:
            vec.tensor_copy(second[:, lo:hi], looked_up("pos2", lo, hi))
        for lo, hi in HALVES:
            vec.tensor_tensor(spread[:, lo:hi], looked_up("pos3", lo, hi), second[:, lo:hi], ALU.subtract)
            nc.scalar.activation(spread_sq[:, lo:hi], spread[:, lo:hi], ACT.Square, scale=root_spread[:])
        for lo, hi in HALVES:
            vec.scalar_tensor_tensor(mid[:, lo:hi], spread[:, lo:hi], 0.5, second[:, lo:hi], ALU.mult, ALU.add)
        for lo, hi in HALVES:
            vec.tensor_tensor(off[:, lo:hi], looked_up("pos1", lo, hi), mid[:, lo:hi], ALU.subtract)
            nc.scalar.activation(off_sq[:, lo:hi], off[:, lo:hi], ACT.Square)
        for lo, hi in HALVES:
            vec.scalar_tensor_tensor(mean[:, lo:hi], off[:, lo:hi], 1.0 / 3.0, mid[:, lo:hi], ALU.mult, ALU.add)
        for lo, hi in THIRDS:
            vec.scalar_tensor_tensor(
                squares[:, lo:hi], spread_sq[:, lo:hi], EPS / VARIANCE_FACTOR, off_sq[:, lo:hi], ALU.add, ALU.add
            )
            nc.scalar.activation(sd[:, lo:hi], squares[:, lo:hi], ACT.Sqrt, scale=VARIANCE_FACTOR)
        for lo, hi in HALVES:
            vec.tensor_tensor(gap[:, lo:hi], hist_sb[:, lo:hi], mean[:, lo:hi], ALU.subtract)

        new_part = mid
        vec.tensor_tensor(new_part[:], looked_up("cen", 0, V), alpha_sb[:], ALU.mult)

        for lo, hi in THIRDS:
            vec.tensor_tensor(capped[:, lo:hi], gap[:, lo:hi], sd[:, lo:hi], ALU.min)
        for lo, hi in THIRDS:
            vec.scalar_tensor_tensor(clamped[:, lo:hi], sd[:, lo:hi], -1.0, capped[:, lo:hi], ALU.mult, ALU.max)
        for lo, hi in THIRDS:
            vec.tensor_tensor(clipped[:, lo:hi], clamped[:, lo:hi], mean[:, lo:hi], ALU.add)
        for lo, hi in THIRDS:
            vec.tensor_tensor(old_part[:, lo:hi], clipped[:, lo:hi], old_share[:, lo:hi], ALU.mult)
        for lo, hi in THIRDS:
            vec.tensor_tensor(result[:, lo:hi], old_part[:, lo:hi], new_part[:, lo:hi], ALU.add)

        for lo, hi in HALVES:
            nc.sync.dma_start(out[:, lo:hi], result[:, lo:hi])
